import numpy as np, ml_dtypes
CORES = [34,162,290,418,42,426]
N = 6
DEG, TK = 3, 512
MASK = [[1,5,0],[1,5,0],[1,5,2],[1,5,3],[1,5,4],[1,5,0]]
def setup_inputs(rng):
    return {"x": rng.standard_normal((N, 128, TK), dtype=np.float32).astype(ml_dtypes.bfloat16), "w": rng.standard_normal((N, 128, DEG * 128), dtype=np.float32).astype(ml_dtypes.bfloat16)}
def setup_inputs_big(rng):
    d = setup_inputs(rng)
    for k in ("x", "w"): d[k] = (d[k].astype(np.float32) * 1024.0).astype(d[k].dtype)
    return d
def setup_inputs_small(rng):
    d = setup_inputs(rng)
    for k in ("x", "w"): d[k] = (d[k].astype(np.float32) * (1 / 1024.0)).astype(d[k].dtype)
    return d
def setup_inputs_apart(rng):
    d = setup_inputs(rng)
    f = (10.0 ** rng.permutation(np.linspace(-1.5, 1.5, N))).astype(np.float32).reshape(N, 1, 1)
    for k in ("x", "w"): d[k] = (d[k].astype(np.float32) * f).astype(d[k].dtype)
    return d
def reference(x, w):
    X, W = x.astype(np.float64), w.astype(np.float64)
    y = np.zeros((N, 128, TK))
    for r in range(N):
        for i, j in enumerate(MASK[r]):
            y[r] += W[r][:, 128 * i:128 * i + 128].T @ X[j]
    return {"y": y.astype(ml_dtypes.bfloat16 if x.dtype != np.float64 else np.float64)}

@@ -1,0 +1,139 @@
+from concourse.bass import DstId, RemoteDMATransfer
+
+P, TK, DEG = 128, 512, 3
+HALF = TK // 2
+
+SCRATCH = {
+    "xs": ("sbuf", [P, TK], "bfloat16"),
+    "ws": ("sbuf", [P, DEG * P], "bfloat16"),
+    "in0": ("sbuf", [P, TK], "bfloat16"),
+    "in1": ("sbuf", [P, TK], "bfloat16"),
+    "in2": ("sbuf", [P, TK], "bfloat16"),
+    "ys": ("sbuf", [P, TK], "bfloat16"),
+    "ps0": ("psum", [P, TK], "float32"),
+    "ps1": ("psum", [P, TK], "float32"),
+}
+SEMAPHORES = ["sx", "sw", "a0", "a1", "a2", "sent", "mm0", "mm1", "cp", "st"]
+
+
+def _bits(m):
+    return bin(m).count("1")
+
+
+def _plan(cores, need, topo):
+    n = len(cores)
+    tiles = sorted({j for r in range(n) for j in need[r] if j != r})
+
+    def one_link(a, b):
+        a, b = cores[a], cores[b]
+        return (topo.mates(a, b) or topo.same_plane(a, b)
+                or (topo.rack(topo.host(a)) != topo.rack(topo.host(b)) and topo.chip(a) == topo.chip(b)))
+
+    calls = {r: [] for r in range(n)}
+    passing = {r: [] for r in range(n)}
+    eta = {}
+    for j in tiles:
+        want = [r for r in range(n) if r != j and j in need[r]]
+        near = [r for r in want if topo.may_write(cores[j], cores[r])]
+        via = {}
+        for r in want:
+            if r in near:
+                continue
+            hubs = [k for k in near if topo.may_write(cores[k], cores[r])]
+            hubs.sort(key=lambda k: (k not in tiles, not one_link(j, k), k))
+            via.setdefault(hubs[0], []).append(r)
+        first = [k for k in near if k in via]
+        rest = [k for k in near if k not in via]
+        t = 0
+        for group in [[k] for k in first] + ([rest] if rest else []):
+            calls[j].append((j, group))
+            for k in group:
+                t += 1
+                eta[(j, k)] = t + (0 if one_link(j, k) else 0.5)
+        for k in first:
+            passing[k].append((eta[(j, k)], j, via[k]))
+    for k in range(n):
+        t = len([1 for c in calls[k] for d in c[1]])
+        for t_in, j, far in sorted(passing[k]):
+            calls[k].append((j, far))
+            t = max(t, t_in + 2)
+            for r in far:
+                t += 1
+                eta[(j, r)] = t
+    return tiles, calls, eta
+
+
+def rank_program(g, core, T, topo):
+    rank = T.rank_of(core)
+    if rank is None:
+        return
+    cores, need, S = T.cores, T.tables["MASK"], T.sem
+    tiles, calls, eta = _plan(cores, need, topo)
+
+    def engines(src, group):
+        m = topo.mask(cores[src], cores[group[0]])
+        for d in group[1:]:
+            m &= topo.mask(cores[src], cores[d])
+        return m
+
+    arrive = {}
+    for s in calls:
+        for j, group in calls[s]:
+            if rank in group:
+                arrive[j] = _bits(engines(s, group))
+
+    def land(j):
+        return T["in%d" % tiles.index(j)]
+
+    def asem(j):
+        return S["a%d" % tiles.index(j)]
+
+    g.sync.dma_start(T.xs[:], T.x[:]).then_inc(S.sx, 16)
+    g.sync.dma_start(T.ws[:], T.w[:]).then_inc(S.sw, 16)
+
+    left = 0
+    for j, group in calls[rank]:
+        if j == rank:
+            g.wait_ge(S.sx, 16)
+            src = T.xs[:]
+        else:
+            g.wait_ge(asem(j), arrive[j])
+            src = land(j)[:]
+        m = engines(rank, group)
+        ids = [topo.addr(cores[d], core) for d in group]
+        if len(group) == 1:
+            g.remote_dma(out_ap=land(j)[:], in_ap=src, remote_sem=asem(j), local_sem=S.sent,
+                         pid=ids[0][1], routing_id=ids[0][0], dma_engine_mask=m)
+        else:
+            g.remote_dma_fused([RemoteDMATransfer(dst_ids=[DstId(rid=a, pnc=b) for a, b in ids], dma_engine_mask=m,
+                                                  remote_sem=asem(j), srcs=[src], dsts=[land(j)[:] for d in group])],
+                               local_sem=S.sent)
+        left += _bits(m)
+    if left:
+        g.wait_ge(S.sent, left)
+
+    order = sorted(range(DEG), key=lambda i: 0 if need[rank][i] == rank else eta[(need[rank][i], rank)])
+    g.tensor.wait_ge(S.sw, 16)
+    for n_done, i in enumerate(order):
+        j = need[rank][i]
+        if j == rank:
+            g.tensor.wait_ge(S.sx, 16)
+            tile = T.xs
+        else:
+            g.tensor.wait_ge(asem(j), arrive[j])
+            tile = land(j)
+        lhsT = T.ws[:, P * i:P * i + P]
+        a = g.tensor.matmul(T.ps0[:, 0:HALF], lhsT, tile[:, 0:HALF], n_done == 0, n_done == DEG - 1)
+        b = g.tensor.matmul(T.ps1[:, 0:HALF], lhsT, tile[:, HALF:TK], n_done == 0, n_done == DEG - 1)
+        if n_done == DEG - 1:
+            a.then_inc(S.mm0, 1)
+            b.then_inc(S.mm1, 1)
+
+    g.vector.wait_ge(S.mm0, 1)
+    g.vector.tensor_copy(T.ys[:, 0:HALF], T.ps0[:, 0:HALF]).then_inc(S.cp, 1)
+    g.vector.wait_ge(S.mm1, 1)
+    g.vector.tensor_copy(T.ys[:, HALF:TK], T.ps1[:, 0:HALF]).then_inc(S.cp, 1)
+
+    g.sync.wait_ge(S.cp, 2)
+    g.sync.dma_start(T.y[:], T.ys[:]).then_inc(S.st, 16)
+    g.sync.wait_ge(S.st, 16)

@@ -16,8 +16,14 @@ SCRATCH = {
 SEMAPHORES = ["sx", "sw", "a0", "a1", "a2", "sent", "mm0", "mm1", "cp", "st"]
 
 
-def _bits(m):
-    return bin(m).count("1")
+def _shares(bits, k):
+    if k == 1:
+        return [bits]
+    if k == 2:
+        return [bits[0::2], bits[1::2]]
+    if k == 3:
+        return [bits[0::2], bits[1::4], bits[3::4]]
+    return [bits[i::4] for i in range(4)]
 
 
 def _plan(cores, need, topo):
@@ -28,6 +34,18 @@ def _plan(cores, need, topo):
         a, b = cores[a], cores[b]
         return (topo.mates(a, b) or topo.same_plane(a, b)
                 or (topo.rack(topo.host(a)) != topo.rack(topo.host(b)) and topo.chip(a) == topo.chip(b)))
+
+    def engines(src, group):
+        m = topo.mask(cores[src], cores[group[0]])
+        for d in group[1:]:
+            m &= topo.mask(cores[src], cores[d])
+        return [1 << b for b in range(16) if m >> b & 1]
+
+    def call(src, j, group, bits):
+        if len(group) == 1:
+            lo, hi = _shares(bits, 2)
+            return (j, [(group[0], lo, 0, HALF), (group[0], hi, HALF, TK)])
+        return (j, [(d, sh, 0, TK) for d, sh in zip(group, _shares(bits, len(group)))])
 
     calls = {r: [] for r in range(n)}
     passing = {r: [] for r in range(n)}
@@ -43,23 +61,24 @@ def _plan(cores, need, topo):
             hubs.sort(key=lambda k: (k not in tiles, not one_link(j, k), k))
             via.setdefault(hubs[0], []).append(r)
         first = [k for k in near if k in via]
-        rest = [k for k in near if k not in via]
+        rest = sorted([k for k in near if k not in via], key=lambda k: (one_link(j, k), k))
         t = 0
         for group in [[k] for k in first] + ([rest] if rest else []):
-            calls[j].append((j, group))
+            calls[j].append(call(j, j, group, engines(j, group)))
+            t += 1
             for k in group:
-                t += 1
                 eta[(j, k)] = t + (0 if one_link(j, k) else 0.5)
         for k in first:
             passing[k].append((eta[(j, k)], j, via[k]))
     for k in range(n):
-        t = len([1 for c in calls[k] for d in c[1]])
-        for t_in, j, far in sorted(passing[k]):
-            calls[k].append((j, far))
-            t = max(t, t_in + 2)
+        if not passing[k]:
+            continue
+        every = [r for t_in, j, far in passing[k] for r in far]
+        parts = _shares(engines(k, every), len(passing[k]))
+        for (t_in, j, far), bits in zip(sorted(passing[k]), parts):
+            calls[k].append(call(k, j, far, bits))
             for r in far:
-                t += 1
-                eta[(j, r)] = t
+                eta[(j, r)] = t_in + 10
     return tiles, calls, eta
 
 
@@ -70,17 +89,12 @@ def rank_program(g, core, T, topo):
     cores, need, S = T.cores, T.tables["MASK"], T.sem
     tiles, calls, eta = _plan(cores, need, topo)
 
-    def engines(src, group):
-        m = topo.mask(cores[src], cores[group[0]])
-        for d in group[1:]:
-            m &= topo.mask(cores[src], cores[d])
-        return m
-
     arrive = {}
     for s in calls:
-        for j, group in calls[s]:
-            if rank in group:
-                arrive[j] = _bits(engines(s, group))
+        for j, parts in calls[s]:
+            for d, bits, c0, c1 in parts:
+                if d == rank:
+                    arrive[j] = arrive.get(j, 0) + len(bits)
 
     def land(j):
         return T["in%d" % tiles.index(j)]
@@ -92,23 +106,20 @@ def rank_program(g, core, T, topo):
     g.sync.dma_start(T.ws[:], T.w[:]).then_inc(S.sw, 16)
 
     left = 0
-    for j, group in calls[rank]:
+    for j, parts in calls[rank]:
         if j == rank:
             g.wait_ge(S.sx, 16)
-            src = T.xs[:]
+            src = T.xs
         else:
             g.wait_ge(asem(j), arrive[j])
-            src = land(j)[:]
-        m = engines(rank, group)
-        ids = [topo.addr(cores[d], core) for d in group]
-        if len(group) == 1:
-            g.remote_dma(out_ap=land(j)[:], in_ap=src, remote_sem=asem(j), local_sem=S.sent,
-                         pid=ids[0][1], routing_id=ids[0][0], dma_engine_mask=m)
-        else:
-            g.remote_dma_fused([RemoteDMATransfer(dst_ids=[DstId(rid=a, pnc=b) for a, b in ids], dma_engine_mask=m,
-                                                  remote_sem=asem(j), srcs=[src], dsts=[land(j)[:] for d in group])],
-                               local_sem=S.sent)
-        left += _bits(m)
+            src = land(j)
+        trs = []
+        for d, bits, c0, c1 in parts:
+            rid, pid = topo.addr(cores[d], core)
+            trs.append(RemoteDMATransfer(dst_ids=[DstId(rid=rid, pnc=pid)], dma_engine_mask=sum(bits), remote_sem=asem(j),
+                                         src=src[:, c0:c1], dst=land(j)[:, c0:c1]))
+            left += len(bits)
+        g.remote_dma_fused(trs, local_sem=S.sent)
     if left:
         g.wait_ge(S.sent, left)
 

@@ -2,6 +2,7 @@ from concourse.bass import DstId, RemoteDMATransfer
 
 P, TK, DEG = 128, 512, 3
 HALF = TK // 2
+COLS = [(0, HALF), (HALF, TK)]
 
 SCRATCH = {
     "xs": ("sbuf", [P, TK], "bfloat16"),
@@ -13,7 +14,7 @@ SCRATCH = {
     "ps0": ("psum", [P, TK], "float32"),
     "ps1": ("psum", [P, TK], "float32"),
 }
-SEMAPHORES = ["sx", "sw", "a0", "a1", "a2", "sent", "mm0", "mm1", "cp", "st"]
+SEMAPHORES = ["sx", "sw", "a00", "a01", "a10", "a11", "a20", "a21", "sent", "mm0", "mm1", "cp0", "cp1", "st"]
 
 
 def _shares(bits, k):
@@ -30,56 +31,41 @@ def _plan(cores, need, topo):
     n = len(cores)
     tiles = sorted({j for r in range(n) for j in need[r] if j != r})
 
-    def one_link(a, b):
-        a, b = cores[a], cores[b]
-        return (topo.mates(a, b) or topo.same_plane(a, b)
-                or (topo.rack(topo.host(a)) != topo.rack(topo.host(b)) and topo.chip(a) == topo.chip(b)))
+    def rack(r):
+        return topo.rack(topo.host(cores[r]))
 
-    def engines(src, group):
+    def cable_only(a, b):
+        return rack(a) != rack(b) and topo.chip(cores[a]) == topo.chip(cores[b])
+
+    def shared(src, group):
         m = topo.mask(cores[src], cores[group[0]])
         for d in group[1:]:
             m &= topo.mask(cores[src], cores[d])
-        return [1 << b for b in range(16) if m >> b & 1]
+        bits = [1 << b for b in range(16) if m >> b & 1]
+        return list(zip(group, _shares(bits, len(group))))
 
-    def call(src, j, group, bits):
-        if len(group) == 1:
-            lo, hi = _shares(bits, 2)
-            return (j, [(group[0], lo, 0, HALF), (group[0], hi, HALF, TK)])
-        return (j, [(d, sh, 0, TK) for d, sh in zip(group, _shares(bits, len(group)))])
-
-    calls = {r: [] for r in range(n)}
-    passing = {r: [] for r in range(n)}
+    own = {r: [] for r in range(n)}
+    fwd = {r: [] for r in range(n)}
     eta = {}
     for j in tiles:
         want = [r for r in range(n) if r != j and j in need[r]]
-        near = [r for r in want if topo.may_write(cores[j], cores[r])]
-        via = {}
-        for r in want:
-            if r in near:
-                continue
-            hubs = [k for k in near if topo.may_write(cores[k], cores[r])]
-            hubs.sort(key=lambda k: (k not in tiles, not one_link(j, k), k))
-            via.setdefault(hubs[0], []).append(r)
-        first = [k for k in near if k in via]
-        rest = sorted([k for k in near if k not in via], key=lambda k: (one_link(j, k), k))
-        t = 0
-        for group in [[k] for k in first] + ([rest] if rest else []):
-            calls[j].append(call(j, j, group, engines(j, group)))
-            t += 1
-            for k in group:
-                eta[(j, k)] = t + (0 if one_link(j, k) else 0.5)
-        for k in first:
-            passing[k].append((eta[(j, k)], j, via[k]))
-    for k in range(n):
-        if not passing[k]:
-            continue
-        every = [r for t_in, j, far in passing[k] for r in far]
-        parts = _shares(engines(k, every), len(passing[k]))
-        for (t_in, j, far), bits in zip(sorted(passing[k]), parts):
-            calls[k].append(call(k, j, far, bits))
-            for r in far:
-                eta[(j, r)] = t_in + 10
-    return tiles, calls, eta
+        home = [r for r in want if rack(r) == rack(j)]
+        away = [r for r in want if rack(r) != rack(j)]
+        group = list(home)
+        for r in home:
+            eta[(j, r)] = 1
+        if away:
+            doors = sorted([r for r in away if topo.may_write(cores[j], cores[r])], key=lambda r: (not cable_only(j, r), r))
+            door = doors[0]
+            group = [door] + home
+            eta[(j, door)] = 2
+            rest = [r for r in away if r != door]
+            if rest:
+                fwd[door].append((j, shared(door, rest)))
+                for r in rest:
+                    eta[(j, r)] = 3
+        own[j].append((j, shared(j, group)))
+    return tiles, {r: own[r] + fwd[r] for r in range(n)}, eta
 
 
 def rank_program(g, core, T, topo):
@@ -87,64 +73,70 @@ def rank_program(g, core, T, topo):
     if rank is None:
         return
     cores, need, S = T.cores, T.tables["MASK"], T.sem
-    tiles, calls, eta = _plan(cores, need, topo)
+    tiles, sends, eta = _plan(cores, need, topo)
 
     arrive = {}
-    for s in calls:
-        for j, parts in calls[s]:
-            for d, bits, c0, c1 in parts:
+    for s in sends:
+        for j, parts in sends[s]:
+            for d, bits in parts:
                 if d == rank:
-                    arrive[j] = arrive.get(j, 0) + len(bits)
+                    arrive[j] = len(bits)
 
     def land(j):
         return T["in%d" % tiles.index(j)]
 
-    def asem(j):
-        return S["a%d" % tiles.index(j)]
+    def asem(j, h):
+        return S["a%d%d" % (tiles.index(j), h)]
 
     g.sync.dma_start(T.xs[:], T.x[:]).then_inc(S.sx, 16)
     g.sync.dma_start(T.ws[:], T.w[:]).then_inc(S.sw, 16)
 
     left = 0
-    for j, parts in calls[rank]:
-        if j == rank:
-            g.wait_ge(S.sx, 16)
-            src = T.xs
-        else:
-            g.wait_ge(asem(j), arrive[j])
-            src = land(j)
-        trs = []
-        for d, bits, c0, c1 in parts:
-            rid, pid = topo.addr(cores[d], core)
-            trs.append(RemoteDMATransfer(dst_ids=[DstId(rid=rid, pnc=pid)], dma_engine_mask=sum(bits), remote_sem=asem(j),
-                                         src=src[:, c0:c1], dst=land(j)[:, c0:c1]))
-            left += len(bits)
-        g.remote_dma_fused(trs, local_sem=S.sent)
+    for j, parts in sends[rank]:
+        for h, (c0, c1) in enumerate(COLS):
+            if j == rank:
+                if h == 0:
+                    g.wait_ge(S.sx, 16)
+                src = T.xs
+            else:
+                g.wait_ge(asem(j, h), arrive[j])
+                src = land(j)
+            trs = []
+            for d, bits in parts:
+                rid, pid = topo.addr(cores[d], core)
+                trs.append(RemoteDMATransfer(dst_ids=[DstId(rid=rid, pnc=pid)], dma_engine_mask=sum(bits),
+                                             remote_sem=asem(j, h), src=src[:, c0:c1], dst=land(j)[:, c0:c1]))
+                left += len(bits)
+            g.remote_dma_fused(trs, local_sem=S.sent)
     if left:
         g.wait_ge(S.sent, left)
 
-    order = sorted(range(DEG), key=lambda i: 0 if need[rank][i] == rank else eta[(need[rank][i], rank)])
+    steps = sorted([(0 if need[rank][i] == rank else eta[(need[rank][i], rank)], h, i) for i in range(DEG) for h in range(2)])
+    done = [0, 0]
+    banks, mms = [T.ps0, T.ps1], [S.mm0, S.mm1]
     g.tensor.wait_ge(S.sw, 16)
-    for n_done, i in enumerate(order):
+    for t, h, i in steps:
         j = need[rank][i]
+        c0, c1 = COLS[h]
         if j == rank:
-            g.tensor.wait_ge(S.sx, 16)
+            if h == 0:
+                g.tensor.wait_ge(S.sx, 16)
             tile = T.xs
         else:
-            g.tensor.wait_ge(asem(j), arrive[j])
+            g.tensor.wait_ge(asem(j, h), arrive[j])
             tile = land(j)
-        lhsT = T.ws[:, P * i:P * i + P]
-        a = g.tensor.matmul(T.ps0[:, 0:HALF], lhsT, tile[:, 0:HALF], n_done == 0, n_done == DEG - 1)
-        b = g.tensor.matmul(T.ps1[:, 0:HALF], lhsT, tile[:, HALF:TK], n_done == 0, n_done == DEG - 1)
-        if n_done == DEG - 1:
-            a.then_inc(S.mm0, 1)
-            b.then_inc(S.mm1, 1)
+        m = g.tensor.matmul(banks[h][:, 0:HALF], T.ws[:, P * i:P * i + P], tile[:, c0:c1], done[h] == 0, done[h] == DEG - 1)
+        done[h] += 1
+        if done[h] == DEG:
+            m.then_inc(mms[h], 1)
 
     g.vector.wait_ge(S.mm0, 1)
-    g.vector.tensor_copy(T.ys[:, 0:HALF], T.ps0[:, 0:HALF]).then_inc(S.cp, 1)
+    g.vector.tensor_copy(T.ys[:, 0:HALF], T.ps0[:, 0:HALF]).then_inc(S.cp0, 1)
     g.vector.wait_ge(S.mm1, 1)
-    g.vector.tensor_copy(T.ys[:, HALF:TK], T.ps1[:, 0:HALF]).then_inc(S.cp, 1)
+    g.vector.tensor_copy(T.ys[:, HALF:TK], T.ps1[:, 0:HALF]).then_inc(S.cp1, 1)
 
-    g.sync.wait_ge(S.cp, 2)
-    g.sync.dma_start(T.y[:], T.ys[:]).then_inc(S.st, 16)
-    g.sync.wait_ge(S.st, 16)
+    g.sync.wait_ge(S.cp0, 1)
+    g.sync.dma_start(T.y[:, 0:HALF], T.ys[:, 0:HALF]).then_inc(S.st, 16)
+    g.sync.wait_ge(S.cp1, 1)
+    g.sync.dma_start(T.y[:, HALF:TK], T.ys[:, HALF:TK]).then_inc(S.st, 16)
+    g.sync.wait_ge(S.st, 32)

@@ -1,8 +1,9 @@
 from concourse.bass import DstId, RemoteDMATransfer
 
 P, TK, DEG = 128, 512, 3
-HALF = TK // 2
-COLS = [(0, HALF), (HALF, TK)]
+WIDTHS = [192, 192, 128]
+COLS = [(sum(WIDTHS[:h]), sum(WIDTHS[:h + 1])) for h in range(len(WIDTHS))]
+NB = len(COLS)
 
 SCRATCH = {
     "xs": ("sbuf", [P, TK], "bfloat16"),
@@ -11,10 +12,11 @@ SCRATCH = {
     "in1": ("sbuf", [P, TK], "bfloat16"),
     "in2": ("sbuf", [P, TK], "bfloat16"),
     "ys": ("sbuf", [P, TK], "bfloat16"),
-    "ps0": ("psum", [P, TK], "float32"),
-    "ps1": ("psum", [P, TK], "float32"),
 }
-SEMAPHORES = ["sx", "sw", "a00", "a01", "a10", "a11", "a20", "a21", "sent", "mm0", "mm1", "cp0", "cp1", "st"]
+SEMAPHORES = ["sx0", "sx1", "sw", "sent", "st"]
+for _h in range(NB):
+    SCRATCH["ps%d" % _h] = ("psum", [P, TK], "float32")
+    SEMAPHORES += ["a0%d" % _h, "a1%d" % _h, "a2%d" % _h, "mm%d" % _h, "cp%d" % _h]
 
 
 def _shares(bits, k):
@@ -88,7 +90,9 @@ def rank_program(g, core, T, topo):
     def asem(j, h):
         return S["a%d%d" % (tiles.index(j), h)]
 
-    g.sync.dma_start(T.xs[:], T.x[:]).then_inc(S.sx, 16)
+    cut = COLS[0][1]
+    g.sync.dma_start(T.xs[:, 0:cut], T.x[:, 0:cut]).then_inc(S.sx0, 16)
+    g.scalar.dma_start(T.xs[:, cut:TK], T.x[:, cut:TK]).then_inc(S.sx1, 16)
     g.sync.dma_start(T.ws[:], T.w[:]).then_inc(S.sw, 16)
 
     left = 0
@@ -96,7 +100,9 @@ def rank_program(g, core, T, topo):
         for h, (c0, c1) in enumerate(COLS):
             if j == rank:
                 if h == 0:
-                    g.wait_ge(S.sx, 16)
+                    g.wait_ge(S.sx0, 16)
+                if h == 1:
+                    g.wait_ge(S.sx1, 16)
                 src = T.xs
             else:
                 g.wait_ge(asem(j, h), arrive[j])
@@ -111,32 +117,29 @@ def rank_program(g, core, T, topo):
     if left:
         g.wait_ge(S.sent, left)
 
-    steps = sorted([(0 if need[rank][i] == rank else eta[(need[rank][i], rank)], h, i) for i in range(DEG) for h in range(2)])
-    done = [0, 0]
-    banks, mms = [T.ps0, T.ps1], [S.mm0, S.mm1]
+    steps = sorted([(0 if need[rank][i] == rank else eta[(need[rank][i], rank)], h, i) for i in range(DEG) for h in range(NB)])
+    done = [0] * NB
     g.tensor.wait_ge(S.sw, 16)
+    g.tensor.wait_ge(S.sx0, 16)
+    g.tensor.wait_ge(S.sx1, 16)
     for t, h, i in steps:
         j = need[rank][i]
         c0, c1 = COLS[h]
         if j == rank:
-            if h == 0:
-                g.tensor.wait_ge(S.sx, 16)
             tile = T.xs
         else:
             g.tensor.wait_ge(asem(j, h), arrive[j])
             tile = land(j)
-        m = g.tensor.matmul(banks[h][:, 0:HALF], T.ws[:, P * i:P * i + P], tile[:, c0:c1], done[h] == 0, done[h] == DEG - 1)
+        m = g.tensor.matmul(T["ps%d" % h][:, 0:c1 - c0], T.ws[:, P * i:P * i + P], tile[:, c0:c1], done[h] == 0, done[h] == DEG - 1)
         done[h] += 1
         if done[h] == DEG:
-            m.then_inc(mms[h], 1)
+            m.then_inc(S["mm%d" % h], 1)
 
-    g.vector.wait_ge(S.mm0, 1)
-    g.vector.tensor_copy(T.ys[:, 0:HALF], T.ps0[:, 0:HALF]).then_inc(S.cp0, 1)
-    g.vector.wait_ge(S.mm1, 1)
-    g.vector.tensor_copy(T.ys[:, HALF:TK], T.ps1[:, 0:HALF]).then_inc(S.cp1, 1)
+    for h, (c0, c1) in enumerate(COLS):
+        g.vector.wait_ge(S["mm%d" % h], 1)
+        g.vector.tensor_copy(T.ys[:, c0:c1], T["ps%d" % h][:, 0:c1 - c0]).then_inc(S["cp%d" % h], 1)
 
-    g.sync.wait_ge(S.cp0, 1)
-    g.sync.dma_start(T.y[:, 0:HALF], T.ys[:, 0:HALF]).then_inc(S.st, 16)
-    g.sync.wait_ge(S.cp1, 1)
-    g.sync.dma_start(T.y[:, HALF:TK], T.ys[:, HALF:TK]).then_inc(S.st, 16)
-    g.sync.wait_ge(S.st, 32)
+    for h, (c0, c1) in enumerate(COLS):
+        g.sync.wait_ge(S["cp%d" % h], 1)
+        g.sync.dma_start(T.y[:, c0:c1], T.ys[:, c0:c1]).then_inc(S.st, 16)
+    g.sync.wait_ge(S.st, 16 * NB)

from concourse.bass import DstId, RemoteDMATransfer

P, TK, DEG = 128, 512, 3
WIDTHS = [192, 192, 128]
COLS = [(sum(WIDTHS[:h]), sum(WIDTHS[:h + 1])) for h in range(len(WIDTHS))]
NB = len(COLS)

SCRATCH = {
    "xs": ("sbuf", [P, TK], "bfloat16"),
    "ws": ("sbuf", [P, DEG * P], "bfloat16"),
    "in0": ("sbuf", [P, TK], "bfloat16"),
    "in1": ("sbuf", [P, TK], "bfloat16"),
    "in2": ("sbuf", [P, TK], "bfloat16"),
    "ys": ("sbuf", [P, TK], "bfloat16"),
}
SEMAPHORES = ["sx0", "sx1", "sw", "sent", "st"]
for _h in range(NB):
    SCRATCH["ps%d" % _h] = ("psum", [P, TK], "float32")
    SEMAPHORES += ["a0%d" % _h, "a1%d" % _h, "a2%d" % _h, "mm%d" % _h, "cp%d" % _h]


def _shares(bits, k):
    if k == 1:
        return [bits]
    if k == 2:
        return [bits[0::2], bits[1::2]]
    if k == 3:
        return [bits[0::2], bits[1::4], bits[3::4]]
    return [bits[i::4] for i in range(4)]


def _plan(cores, need, topo):
    n = len(cores)
    tiles = sorted({j for r in range(n) for j in need[r] if j != r})

    def rack(r):
        return topo.rack(topo.host(cores[r]))

    def cable_only(a, b):
        return rack(a) != rack(b) and topo.chip(cores[a]) == topo.chip(cores[b])

    def shared(src, group):
        m = topo.mask(cores[src], cores[group[0]])
        for d in group[1:]:
            m &= topo.mask(cores[src], cores[d])
        bits = [1 << b for b in range(16) if m >> b & 1]
        return list(zip(group, _shares(bits, len(group))))

    own = {r: [] for r in range(n)}
    fwd = {r: [] for r in range(n)}
    eta = {}
    for j in tiles:
        want = [r for r in range(n) if r != j and j in need[r]]
        home = [r for r in want if rack(r) == rack(j)]
        away = [r for r in want if rack(r) != rack(j)]
        group = list(home)
        for r in home:
            eta[(j, r)] = 1
        if away:
            doors = sorted([r for r in away if topo.may_write(cores[j], cores[r])], key=lambda r: (not cable_only(j, r), r))
            door = doors[0]
            group = [door] + home
            eta[(j, door)] = 2
            rest = [r for r in away if r != door]
            if rest:
                fwd[door].append((j, shared(door, rest)))
                for r in rest:
                    eta[(j, r)] = 3
        own[j].append((j, shared(j, group)))
    return tiles, {r: own[r] + fwd[r] for r in range(n)}, eta


def rank_program(g, core, T, topo):
    rank = T.rank_of(core)
    if rank is None:
        return
    cores, need, S = T.cores, T.tables["MASK"], T.sem
    tiles, sends, eta = _plan(cores, need, topo)

    arrive = {}
    for s in sends:
        for j, parts in sends[s]:
            for d, bits in parts:
                if d == rank:
                    arrive[j] = len(bits)

    def land(j):
        return T["in%d" % tiles.index(j)]

    def asem(j, h):
        return S["a%d%d" % (tiles.index(j), h)]

    cut = COLS[0][1]
    g.sync.dma_start(T.xs[:, 0:cut], T.x[:, 0:cut]).then_inc(S.sx0, 16)
    g.scalar.dma_start(T.xs[:, cut:TK], T.x[:, cut:TK]).then_inc(S.sx1, 16)
    g.sync.dma_start(T.ws[:], T.w[:]).then_inc(S.sw, 16)

    left = 0
    for j, parts in sends[rank]:
        for h, (c0, c1) in enumerate(COLS):
            if j == rank:
                if h == 0:
                    g.wait_ge(S.sx0, 16)
                if h == 1:
                    g.wait_ge(S.sx1, 16)
                src = T.xs
            else:
                g.wait_ge(asem(j, h), arrive[j])
                src = land(j)
            trs = []
            for d, bits in parts:
                rid, pid = topo.addr(cores[d], core)
                trs.append(RemoteDMATransfer(dst_ids=[DstId(rid=rid, pnc=pid)], dma_engine_mask=sum(bits),
                                             remote_sem=asem(j, h), src=src[:, c0:c1], dst=land(j)[:, c0:c1]))
                left += len(bits)
            g.remote_dma_fused(trs, local_sem=S.sent)
    if left:
        g.wait_ge(S.sent, left)

    steps = sorted([(0 if need[rank][i] == rank else eta[(need[rank][i], rank)], h, i) for i in range(DEG) for h in range(NB)])
    done = [0] * NB
    g.tensor.wait_ge(S.sw, 16)
    g.tensor.wait_ge(S.sx0, 16)
    g.tensor.wait_ge(S.sx1, 16)
    for t, h, i in steps:
        j = need[rank][i]
        c0, c1 = COLS[h]
        if j == rank:
            tile = T.xs
        else:
            g.tensor.wait_ge(asem(j, h), arrive[j])
            tile = land(j)
        m = g.tensor.matmul(T["ps%d" % h][:, 0:c1 - c0], T.ws[:, P * i:P * i + P], tile[:, c0:c1], done[h] == 0, done[h] == DEG - 1)
        done[h] += 1
        if done[h] == DEG:
            m.then_inc(S["mm%d" % h], 1)

    for h, (c0, c1) in enumerate(COLS):
        g.vector.wait_ge(S["mm%d" % h], 1)
        g.vector.tensor_copy(T.ys[:, c0:c1], T["ps%d" % h][:, 0:c1 - c0]).then_inc(S["cp%d" % h], 1)

    for h, (c0, c1) in enumerate(COLS):
        g.sync.wait_ge(S["cp%d" % h], 1)
        g.sync.dma_start(T.y[:, c0:c1], T.ys[:, c0:c1]).then_inc(S.st, 16)
    g.sync.wait_ge(S.st, 16 * NB)
